import numpy as np
import ml_dtypes


def mxq(x, axis, fmt="e4m3"):
    dtype, down = {"e4m3": (ml_dtypes.float8_e4m3fn, 7), "e5m2": (ml_dtypes.float8_e5m2, 14)}[fmt]
    v = np.moveaxis(np.asarray(x, np.float32).astype(ml_dtypes.bfloat16).astype(np.float64), axis, -1)
    blocks = v.reshape(v.shape[:-1] + (-1, 32))
    amax = np.abs(blocks).max(-1, keepdims=True)
    byte = np.maximum(np.where(amax > 0, np.frexp(amax)[1] - 1 + 127, 0) - down, 1)
    scale = np.exp2(byte - 127.0)
    codes = (blocks / scale).astype(np.float32).astype(dtype).astype(np.float64)
    return np.moveaxis((codes * scale).reshape(v.shape), -1, axis)


WIDE = False


def mx_kscale(k):
    if not WIDE:
        return np.ones(k)
    levels = np.array([10, -10, 5, -5, 0])
    if k % 512:
        return np.exp2(np.random.permutation(np.resize(levels, k // 32))).repeat(32)
    a = np.empty((k // 512, 16))
    for p in range(k // 512):
        a[p, :8] = np.random.permutation(np.resize(levels, 8))
        for g in range(8):
            far = levels[np.abs(levels - a[p, g]) >= 10]
            a[p, g + 8] = far[np.random.randint(len(far))]
    return np.exp2(a.ravel()).repeat(32)


def f64(x):
    return np.asarray(x).astype(np.float64)


def striped(idx):
    return np.tile(idx.reshape(-1, 16).T, (8, 1)).astype(np.uint16)


def unstriped(offs):
    return offs[:16].T.reshape(-1).astype(np.int64)


def pack_weight(w):
    k, n = w.shape
    w = f64(np.asarray(w, np.float32).astype(ml_dtypes.bfloat16)).reshape(k // 32, 32, n)
    amax = np.abs(w).max(1)
    byte = np.clip(np.where(amax > 0, np.frexp(amax)[1] - 1 + 127 - 7, 1), 1, 254)
    scaled = (w * np.exp2(127.0 - byte)[:, None, :]).reshape(k, n).astype(np.float32)
    words = np.ascontiguousarray(scaled.reshape(k // 512, 128, 4, n).transpose(0, 1, 3, 2)).astype(ml_dtypes.float8_e4m3fn).view(np.uint8)
    return words, np.ascontiguousarray(byte.astype(np.uint8).reshape(k // 512, 16, n))


def unpack_weight(words, scales):
    g, p, n, _ = words.shape
    vals = np.ascontiguousarray(words).view(ml_dtypes.float8_e4m3fn).astype(np.float64) * np.repeat(np.exp2(scales.astype(np.float64) - 127.0), 8, axis=1)[..., None]
    return vals.transpose(0, 1, 3, 2).reshape(g * 512, n)


def sigmoid(v):
    return 1.0 / (1.0 + np.exp(-np.maximum(v, -700.0)))


K, T, S, H, N = 512, 2048, 512, 512, 128


def setup_inputs():
    n = np.random.standard_normal
    s = mx_kscale(K)[:, None]
    u = mx_kscale(H)
    packed_xT = pack_weight(n((K, T)) * s)
    return {
        "x_words": packed_xT[0],
        "x_scales": packed_xT[1],
        "w1": (n((K, H)) / np.sqrt(K) / s).astype(np.float32),
        "w2": (n((K, H)) / np.sqrt(K) / s).astype(np.float32),
        "unit": (np.random.uniform(0.7, 1.3, (H, 1)) * u[:, None]).astype(np.float32),
        "ta": (n((H, N)) / np.sqrt(2 * H) / u[:, None]).astype(np.float32),
        "offs": striped(np.random.permutation(T)[:S]),
    }


def reference(x_words, x_scales, w1, w2, unit, ta, offs):
    xq = unpack_weight(x_words, x_scales)[:, unstriped(offs)]
    mm = mxq(f64(w1), 0, "e4m3").T @ xq
    sd = np.exp(0.4 * ((mxq(f64(w2), 0, "e4m3").T @ xq)))
    a = mm / sd
    pr = sigmoid(1.702 * a)
    f = 0.3989 * (np.exp(-0.5 * ((a) ** 2)))
    m1 = mm * pr + sd * f
    zta = f64(unit) * m1
    return mxq(f64(ta), 0, "e4m3").T @ mxq(zta, 0, "e4m3")

@@ -1,0 +1,196 @@
+import math
+from contextlib import ExitStack
+
+import concourse.mybir as mybir
+from concourse.masks import make_identity
+
+K, T, S, H, N = 512, 2048, 512, 512, 128
+FLOPS = 2 * K * H * S * 2 + 2 * H * N * S
+
+F32 = mybir.dt.float32
+BF16 = mybir.dt.bfloat16
+I32 = mybir.dt.int32
+U32 = mybir.dt.uint32
+U16 = mybir.dt.uint16
+U8 = mybir.dt.uint8
+FP8X4 = mybir.dt.float8_e4m3fn_x4
+ACT = mybir.ActivationFunctionType
+ALU = mybir.AluOpType
+
+P = 128
+PACK = 4
+HALF_UNITS = H // 2
+HALF_TOKENS = S // 2
+
+
+def tile_picked_yadf_mean_p_kernel(tc, x_words, x_scales, w1, w2, unit, ta, offs, out):
+    nc = tc.nc
+    with ExitStack() as ctx:
+        keep = ctx.enter_context(tc.tile_pool(name="keep", bufs=1))
+        work = ctx.enter_context(tc.tile_pool(name="work", bufs=3))
+        psum = ctx.enter_context(tc.psum_pool(name="psum", bufs=3))
+
+        offsets = keep.tile([P, S // 16], U16, name="offsets")
+        word_window = keep.tile([P, T], I32, name="word_window", align_bytes=64)
+        scale_window = keep.tile([P, T], U8, name="scale_window", align_bytes=64)
+        nc.vector.memset(scale_window[:].bitcast(I32), 0)
+        nc.sync.dma_start(offsets[:], offs)
+        nc.sync.dma_start(word_window[:], x_words[0].rearrange("p n t -> p (n t)").bitcast(I32))
+        for q in range(4):
+            nc.scalar.dma_start(
+                scale_window[32 * q : 32 * q + 4, :].bitcast(I32),
+                x_scales[0, 4 * q : 4 * q + 4, :].bitcast(I32),
+            )
+
+        raw = {}
+        for c in range(2):
+            for name, w in (("dev", w2), ("mean", w1)):
+                raw[name, c] = keep.tile([P, PACK, HALF_UNITS], F32, name="raw_%s%d" % (name, c))
+                nc.sync.dma_start(
+                    raw[name, c][:],
+                    w[:, c * HALF_UNITS : (c + 1) * HALF_UNITS].rearrange("(p j) c -> p j c", j=PACK),
+                )
+        ta_raw = keep.tile([P, PACK, N], F32, name="ta_raw")
+        nc.sync.dma_start(ta_raw[:], ta.rearrange("(p j) c -> p j c", j=PACK))
+        unit_raw = keep.tile([P, 1, PACK], F32, name="unit_raw")
+        nc.sync.dma_start(unit_raw[:, 0, :], unit.rearrange("(p t) o -> p (t o)", t=PACK))
+
+        identity = keep.tile([P, P], F32, name="identity")
+        make_identity(nc, identity[:])
+
+        def cast_weights(name, c, engine):
+            grouped = keep.tile([P, PACK * HALF_UNITS], BF16, name="grouped_%s%d" % (name, c), align_bytes=64)
+            dst = grouped[:].rearrange("p (t m j) -> p m j t", t=PACK, j=PACK)
+            src = raw[name, c][:].rearrange("p j (m t) -> p m j t", t=PACK)
+            if engine == "scalar":
+                nc.scalar.activation(dst, src, ACT.Copy)
+            elif engine == "vector":
+                nc.vector.tensor_copy(dst, src)
+            else:
+                nc.gpsimd.tensor_scalar(dst, src, 1.0, 0.0, ALU.mult, ALU.add)
+            return grouped
+
+        def quantise(grouped, name):
+            width = grouped.shape[1] // PACK
+            codes = keep.tile([P, width], U32, name="codes_" + name, align_bytes=64)
+            scales = keep.tile([P, width], U8, name="scales_" + name, align_bytes=64)
+            nc.vector.quantize_mx(out=codes[:].bitcast(FP8X4), scales=scales[:], in_=grouped)
+            return codes, scales
+
+        picked = []
+        for h in range(2):
+            entries = offsets[:, h * (HALF_TOKENS // 16) : (h + 1) * (HALF_TOKENS // 16)]
+            words = keep.tile([P, HALF_TOKENS], U32, name="x_codes%d" % h, align_bytes=64)
+            scales = keep.tile([P, HALF_TOKENS], U8, name="x_scales%d" % h, align_bytes=64)
+            nc.vector.tensor_copy(words[:], word_window[:].bitcast(U32).indirect(entries))
+            nc.vector.tensor_copy(scales[:], scale_window[:].indirect(entries))
+            picked.append((words, scales))
+
+        weights = {}
+        weights["dev", 0] = quantise(cast_weights("dev", 0, "scalar")[:], "dev0")
+        weights["mean", 0] = quantise(cast_weights("mean", 0, "vector")[:], "mean0")
+        grouped_dev1 = cast_weights("dev", 1, "scalar")
+        grouped_mean1 = cast_weights("mean", 1, "vector")
+        ta_grouped = keep.tile([P, PACK * N], BF16, name="ta_grouped", align_bytes=64)
+        nc.scalar.activation(
+            ta_grouped[:].rearrange("p (c i j) -> p c j i", i=4, j=PACK),
+            ta_raw[:].rearrange("p j (c i) -> p c j i", i=4),
+            ACT.Copy,
+        )
+
+        gated = [keep.tile([P, 2, PACK, P], F32, name="gated%d" % h) for h in range(2)]
+        bump = [keep.tile([P, 2, PACK, P], F32, name="bump%d" % h) for h in range(2)]
+
+        def product(name, c, h):
+            bank = psum.tile([P, 2 * HALF_UNITS], F32, name="bank_" + name, tag=name)
+            codes, scales = weights[name, c]
+            words, word_scales = picked[h]
+            for i in range(2):
+                nc.tensor.matmul_mx(
+                    out=bank[:, i * HALF_UNITS : (i + 1) * HALF_UNITS],
+                    lhsT=words[:, i * P : (i + 1) * P].bitcast(FP8X4),
+                    lhsT_scale=word_scales[:, i * P : (i + 1) * P],
+                    rhs=codes[:].bitcast(FP8X4),
+                    rhs_scale=scales[:],
+                    start=True,
+                    stop=True,
+                )
+            return bank
+
+        def step(c, h):
+            width = 2 * HALF_UNITS
+            m = HALF_UNITS // PACK
+            dev = product("dev", c, h)
+            mean = product("mean", c, h)
+            inv_sd = work.tile([P, width], F32, name="inv_sd")
+            nc.scalar.activation(inv_sd[:], dev[:], ACT.Exp, scale=-0.4)
+            a = work.tile([P, width], F32, name="a")
+            nc.vector.tensor_tensor(a[:], mean[:], inv_sd[:], ALU.mult)
+            a_sq = work.tile([P, width], F32, name="a_sq")
+            nc.scalar.activation(a_sq[:], a[:], ACT.Square)
+            th = work.tile([P, width], F32, name="th")
+            nc.scalar.activation(th[:], a[:], ACT.Tanh, scale=0.851)
+            arg = work.tile([P, width], F32, name="arg")
+            nc.vector.scalar_tensor_tensor(arg[:], a_sq[:], -1.25, dev[:], ALU.mult, ALU.add)
+            nc.vector.scalar_tensor_tensor(
+                gated[h][:, :, :, c * m : (c + 1) * m].rearrange("p b t m -> p (b t) m"),
+                th[:].rearrange("p (r m) -> p r m", m=m),
+                1.0,
+                mean[:].rearrange("p (r m) -> p r m", m=m),
+                ALU.add,
+                ALU.mult,
+            )
+            nc.scalar.activation(
+                bump[h][:, :, :, c * m : (c + 1) * m].rearrange("p b t m -> p (b t) m"),
+                arg[:].rearrange("p (r m) -> p r m", m=m),
+                ACT.Exp,
+                bias=math.log(2.0 * 0.3989),
+                scale=0.4,
+            )
+
+        def turn(h, i, hidden):
+            turned = psum.tile([P, PACK, P], F32, name="turned", tag="turned", bufs=2)
+            for t in range(PACK):
+                nc.tensor.matmul(turned[:, t, :], gated[h][:, i, t, :], identity[:], start=True, stop=False, is_transpose=True)
+                nc.tensor.matmul(turned[:, t, :], bump[h][:, i, t, :], identity[:], start=False, stop=True, is_transpose=True)
+            nc.vector.scalar_tensor_tensor(
+                hidden.rearrange("p (n t) -> p n t", t=PACK),
+                turned[:].rearrange("p t n -> p n t"),
+                0.5,
+                unit_raw[:].to_broadcast([P, P, PACK]),
+                ALU.mult,
+                ALU.mult,
+            )
+
+        def head(hidden, first, name):
+            width = hidden.shape[1] // PACK
+            codes, scales = quantise(hidden, name)
+            bank = psum.tile([P, width], F32, name="bank_out", tag="dev")
+            nc.tensor.matmul_mx(
+                out=bank[:],
+                lhsT=ta_codes[:].bitcast(FP8X4),
+                lhsT_scale=ta_scales[:],
+                rhs=codes[:].bitcast(FP8X4),
+                rhs_scale=scales[:],
+                start=True,
+                stop=True,
+            )
+            result = keep.tile([P, width], F32, name="result_" + name)
+            nc.scalar.copy(result[:], bank[:])
+            nc.sync.dma_start(out[:, first : first + width], result[:])
+
+        step(0, 0)
+        step(0, 1)
+        weights["dev", 1] = quantise(grouped_dev1[:], "dev1")
+        weights["mean", 1] = quantise(grouped_mean1[:], "mean1")
+        step(1, 0)
+        ta_codes, ta_scales = quantise(ta_grouped[:], "ta")
+        step(1, 1)
+        hidden0 = keep.tile([P, 2 * PACK * P], BF16, name="hidden0", align_bytes=64)
+        for i in range(2):
+            turn(0, i, hidden0[:, i * PACK * P : (i + 1) * PACK * P])
+        head(hidden0[:], 0, "z0")
+        for i in range(2):
+            hidden1 = keep.tile([P, PACK * P], BF16, name="hidden1_%d" % i, align_bytes=64)
+            turn(1, i, hidden1[:])
+            head(hidden1[:], HALF_TOKENS + i * P, "z1_%d" % i)

@@ -21,35 +21,41 @@ P = 128
 PACK = 4
 HALF_UNITS = H // 2
 HALF_TOKENS = S // 2
+BLOCKS = S // P
+LAST = BLOCKS - 1
 
 
 def tile_picked_yadf_mean_p_kernel(tc, x_words, x_scales, w1, w2, unit, ta, offs, out):
     nc = tc.nc
     with ExitStack() as ctx:
         keep = ctx.enter_context(tc.tile_pool(name="keep", bufs=1))
-        work = ctx.enter_context(tc.tile_pool(name="work", bufs=3))
+        work = ctx.enter_context(tc.tile_pool(name="work", bufs=4))
         psum = ctx.enter_context(tc.psum_pool(name="psum", bufs=3))
 
         offsets = keep.tile([P, S // 16], U16, name="offsets")
         word_window = keep.tile([P, T], I32, name="word_window", align_bytes=64)
         scale_window = keep.tile([P, T], U8, name="scale_window", align_bytes=64)
-        nc.vector.memset(scale_window[:].bitcast(I32), 0)
-        nc.sync.dma_start(offsets[:], offs)
-        nc.sync.dma_start(word_window[:], x_words[0].rearrange("p n t -> p (n t)").bitcast(I32))
-        for q in range(4):
-            nc.scalar.dma_start(
-                scale_window[32 * q : 32 * q + 4, :].bitcast(I32),
-                x_scales[0, 4 * q : 4 * q + 4, :].bitcast(I32),
-            )
+        nc.gpsimd.memset(scale_window[:].bitcast(I32), 0)
 
         raw = {}
-        for c in range(2):
-            for name, w in (("dev", w2), ("mean", w1)):
+
+        def load_weights(name, w):
+            for c in range(2):
                 raw[name, c] = keep.tile([P, PACK, HALF_UNITS], F32, name="raw_%s%d" % (name, c))
                 nc.sync.dma_start(
                     raw[name, c][:],
                     w[:, c * HALF_UNITS : (c + 1) * HALF_UNITS].rearrange("(p j) c -> p j c", j=PACK),
                 )
+
+        nc.sync.dma_start(offsets[:], offs)
+        nc.sync.dma_start(word_window[:], x_words[0].rearrange("p n t -> p (n t)").bitcast(I32))
+        for q in range(4):
+            nc.sync.dma_start(
+                scale_window[32 * q : 32 * q + 4, :].bitcast(I32),
+                x_scales[0, 4 * q : 4 * q + 4, :].bitcast(I32),
+            )
+        load_weights("dev", w2)
+        load_weights("mean", w1)
         ta_raw = keep.tile([P, PACK, N], F32, name="ta_raw")
         nc.sync.dma_start(ta_raw[:], ta.rearrange("(p j) c -> p j c", j=PACK))
         unit_raw = keep.tile([P, 1, PACK], F32, name="unit_raw")
@@ -58,17 +64,14 @@ def tile_picked_yadf_mean_p_kernel(tc, x_words, x_scales, w1, w2, unit, ta, offs
         identity = keep.tile([P, P], F32, name="identity")
         make_identity(nc, identity[:])
 
-        def cast_weights(name, c, engine):
-            grouped = keep.tile([P, PACK * HALF_UNITS], BF16, name="grouped_%s%d" % (name, c), align_bytes=64)
-            dst = grouped[:].rearrange("p (t m j) -> p m j t", t=PACK, j=PACK)
+        def cast_weights(grouped, name, c, on_scalar):
+            m = HALF_UNITS // PACK
+            dst = grouped[:].rearrange("p (t m j) -> p m j t", t=PACK, j=PACK)[:, c * m : (c + 1) * m]
             src = raw[name, c][:].rearrange("p j (m t) -> p m j t", t=PACK)
-            if engine == "scalar":
+            if on_scalar:
                 nc.scalar.activation(dst, src, ACT.Copy)
-            elif engine == "vector":
-                nc.vector.tensor_copy(dst, src)
             else:
-                nc.gpsimd.tensor_scalar(dst, src, 1.0, 0.0, ALU.mult, ALU.add)
-            return grouped
+                nc.vector.tensor_copy(dst, src)
 
         def quantise(grouped, name):
             width = grouped.shape[1] // PACK
@@ -76,6 +79,17 @@ def tile_picked_yadf_mean_p_kernel(tc, x_words, x_scales, w1, w2, unit, ta, offs
             scales = keep.tile([P, width], U8, name="scales_" + name, align_bytes=64)
             nc.vector.quantize_mx(out=codes[:].bitcast(FP8X4), scales=scales[:], in_=grouped)
             return codes, scales
+
+        def product(bank, lhs, lhs_cols, rhs, rhs_cols):
+            nc.tensor.matmul_mx(
+                out=bank,
+                lhsT=lhs[0][:, lhs_cols].bitcast(FP8X4),
+                lhsT_scale=lhs[1][:, lhs_cols],
+                rhs=rhs[0][:, rhs_cols].bitcast(FP8X4),
+                rhs_scale=rhs[1][:, rhs_cols],
+                start=True,
+                stop=True,
+            )
 
         picked = []
         for h in range(2):
@@ -87,75 +101,64 @@ def tile_picked_yadf_mean_p_kernel(tc, x_words, x_scales, w1, w2, unit, ta, offs
             picked.append((words, scales))
 
         weights = {}
-        weights["dev", 0] = quantise(cast_weights("dev", 0, "scalar")[:], "dev0")
-        weights["mean", 0] = quantise(cast_weights("mean", 0, "vector")[:], "mean0")
-        grouped_dev1 = cast_weights("dev", 1, "scalar")
-        grouped_mean1 = cast_weights("mean", 1, "vector")
-        ta_grouped = keep.tile([P, PACK * N], BF16, name="ta_grouped", align_bytes=64)
-        nc.scalar.activation(
-            ta_grouped[:].rearrange("p (c i j) -> p c j i", i=4, j=PACK),
-            ta_raw[:].rearrange("p j (c i) -> p c j i", i=4),
-            ACT.Copy,
-        )
+        grouped_dev = keep.tile([P, PACK * H], BF16, name="grouped_dev", tag="grouped", align_bytes=64)
+        cast_weights(grouped_dev, "dev", 0, True)
+        cast_weights(grouped_dev, "dev", 1, False)
+        weights["dev"] = quantise(grouped_dev[:], "dev")
 
-        gated = [keep.tile([P, 2, PACK, P], F32, name="gated%d" % h) for h in range(2)]
-        bump = [keep.tile([P, 2, PACK, P], F32, name="bump%d" % h) for h in range(2)]
+        held = {}
 
-        def product(name, c, h):
-            bank = psum.tile([P, 2 * HALF_UNITS], F32, name="bank_" + name, tag=name)
-            codes, scales = weights[name, c]
-            words, word_scales = picked[h]
-            for i in range(2):
-                nc.tensor.matmul_mx(
-                    out=bank[:, i * HALF_UNITS : (i + 1) * HALF_UNITS],
-                    lhsT=words[:, i * P : (i + 1) * P].bitcast(FP8X4),
-                    lhsT_scale=word_scales[:, i * P : (i + 1) * P],
-                    rhs=codes[:].bitcast(FP8X4),
-                    rhs_scale=scales[:],
-                    start=True,
-                    stop=True,
-                )
-            return bank
+        def first_layer(name, b):
+            bank = psum.tile([P, H], F32, name="bank_" + name, tag=name)
+            tokens = slice((b % 2) * P, (b % 2 + 1) * P)
+            if b == LAST:
+                for t in range(PACK):
+                    product(bank[:, t * P : (t + 1) * P], weights[name], slice(t * P, (t + 1) * P), picked[b // 2], tokens)
+                held[name, b] = bank[:].rearrange("p (t n) -> p n t", t=PACK)
+            else:
+                product(bank[:], picked[b // 2], tokens, weights[name], slice(0, H))
+                held[name, b] = bank[:].rearrange("p (n t) -> p n t", t=PACK)
 
-        def step(c, h):
-            width = 2 * HALF_UNITS
-            m = HALF_UNITS // PACK
-            dev = product("dev", c, h)
-            mean = product("mean", c, h)
-            inv_sd = work.tile([P, width], F32, name="inv_sd")
-            nc.scalar.activation(inv_sd[:], dev[:], ACT.Exp, scale=-0.4)
-            a = work.tile([P, width], F32, name="a")
-            nc.vector.tensor_tensor(a[:], mean[:], inv_sd[:], ALU.mult)
-            a_sq = work.tile([P, width], F32, name="a_sq")
-            nc.scalar.activation(a_sq[:], a[:], ACT.Square)
-            th = work.tile([P, width], F32, name="th")
-            nc.scalar.activation(th[:], a[:], ACT.Tanh, scale=0.851)
-            arg = work.tile([P, width], F32, name="arg")
-            nc.vector.scalar_tensor_tensor(arg[:], a_sq[:], -1.25, dev[:], ALU.mult, ALU.add)
-            nc.vector.scalar_tensor_tensor(
-                gated[h][:, :, :, c * m : (c + 1) * m].rearrange("p b t m -> p (b t) m"),
-                th[:].rearrange("p (r m) -> p r m", m=m),
-                1.0,
-                mean[:].rearrange("p (r m) -> p r m", m=m),
-                ALU.add,
-                ALU.mult,
-            )
-            nc.scalar.activation(
-                bump[h][:, :, :, c * m : (c + 1) * m].rearrange("p b t m -> p (b t) m"),
-                arg[:].rearrange("p (r m) -> p r m", m=m),
-                ACT.Exp,
-                bias=math.log(2.0 * 0.3989),
-                scale=0.4,
-            )
+        def fresh(name, b):
+            tile = work.tile([P, P, PACK], F32, name=name, tag=name)
+            held[name, b] = tile[:]
+            return held[name, b]
 
-        def turn(h, i, hidden):
+        def inverse_deviation(b):
+            first_layer("dev", b)
+            nc.scalar.activation(fresh("inv_sd", b), held["dev", b], ACT.Exp, scale=-0.4)
+
+        def ratio(b):
+            first_layer("mean", b)
+            nc.vector.tensor_tensor(fresh("a", b), held["mean", b], held["inv_sd", b], ALU.mult)
+
+        def square_and_tanh(b):
+            nc.scalar.activation(fresh("a_sq", b), held["a", b], ACT.Square)
+            nc.scalar.activation(fresh("th", b), held["a", b], ACT.Tanh, scale=0.851)
+
+        def terms(b):
+            nc.vector.scalar_tensor_tensor(fresh("arg", b), held["a_sq", b], -1.25, held["dev", b], ALU.mult, ALU.add)
+            nc.vector.scalar_tensor_tensor(fresh("gated", b), held["th", b], 1.0, held["mean", b], ALU.add, ALU.mult)
+            nc.scalar.activation(fresh("bump", b), held["arg", b], ACT.Exp, bias=math.log(2.0 * 0.3989), scale=0.4)
+
+        def add_terms(b):
+            if b == LAST:
+                nc.vector.tensor_tensor(fresh("total", b), held["gated", b], held["bump", b], ALU.add)
+                return
             turned = psum.tile([P, PACK, P], F32, name="turned", tag="turned", bufs=2)
-            for t in range(PACK):
-                nc.tensor.matmul(turned[:, t, :], gated[h][:, i, t, :], identity[:], start=True, stop=False, is_transpose=True)
-                nc.tensor.matmul(turned[:, t, :], bump[h][:, i, t, :], identity[:], start=False, stop=True, is_transpose=True)
+            for k, name in enumerate(("gated", "bump")):
+                columns = held[name, b].rearrange("p n t -> p (n t)")
+                for t in range(PACK):
+                    nc.tensor.matmul(
+                        turned[:, t, :], columns[:, t * P : (t + 1) * P], identity[:],
+                        start=(k == 0 and t == 0), stop=(k == 1 and t == PACK - 1), is_transpose=True,
+                    )
+            held["total", b] = turned[:].rearrange("p t n -> p n t")
+
+        def scale_by_unit(b, hidden):
             nc.vector.scalar_tensor_tensor(
                 hidden.rearrange("p (n t) -> p n t", t=PACK),
-                turned[:].rearrange("p t n -> p n t"),
+                held["total", b],
                 0.5,
                 unit_raw[:].to_broadcast([P, P, PACK]),
                 ALU.mult,
@@ -164,33 +167,52 @@ def tile_picked_yadf_mean_p_kernel(tc, x_words, x_scales, w1, w2, unit, ta, offs
 
         def head(hidden, first, name):
             width = hidden.shape[1] // PACK
-            codes, scales = quantise(hidden, name)
+            quantised = quantise(hidden, name)
             bank = psum.tile([P, width], F32, name="bank_out", tag="dev")
-            nc.tensor.matmul_mx(
-                out=bank[:],
-                lhsT=ta_codes[:].bitcast(FP8X4),
-                lhsT_scale=ta_scales[:],
-                rhs=codes[:].bitcast(FP8X4),
-                rhs_scale=scales[:],
-                start=True,
-                stop=True,
-            )
+            product(bank[:], weights["ta"], slice(0, N), quantised, slice(0, width))
             result = keep.tile([P, width], F32, name="result_" + name)
             nc.scalar.copy(result[:], bank[:])
             nc.sync.dma_start(out[:, first : first + width], result[:])
 
-        step(0, 0)
-        step(0, 1)
-        weights["dev", 1] = quantise(grouped_dev1[:], "dev1")
-        weights["mean", 1] = quantise(grouped_mean1[:], "mean1")
-        step(1, 0)
-        ta_codes, ta_scales = quantise(ta_grouped[:], "ta")
-        step(1, 1)
-        hidden0 = keep.tile([P, 2 * PACK * P], BF16, name="hidden0", align_bytes=64)
-        for i in range(2):
-            turn(0, i, hidden0[:, i * PACK * P : (i + 1) * PACK * P])
-        head(hidden0[:], 0, "z0")
-        for i in range(2):
-            hidden1 = keep.tile([P, PACK * P], BF16, name="hidden1_%d" % i, align_bytes=64)
-            turn(1, i, hidden1[:])
-            head(hidden1[:], HALF_TOKENS + i * P, "z1_%d" % i)
+        grouped_mean = keep.tile([P, PACK * H], BF16, name="grouped_mean", tag="grouped", align_bytes=64)
+        hidden01 = keep.tile([P, 2 * H], BF16, name="hidden01", align_bytes=64)
+        hidden2 = keep.tile([P, H], BF16, name="hidden2", align_bytes=64)
+        hidden3 = keep.tile([P, H], BF16, name="hidden3", align_bytes=64)
+        ta_grouped = keep.tile([P, PACK * N], BF16, name="ta_grouped", align_bytes=64)
+
+        cast_weights(grouped_mean, "mean", 0, True)
+        cast_weights(grouped_mean, "mean", 1, False)
+        weights["mean"] = quantise(grouped_mean[:], "mean")
+        inverse_deviation(0)
+        inverse_deviation(1)
+        inverse_deviation(2)
+        ratio(0)
+        ratio(1)
+        square_and_tanh(0)
+        terms(0)
+        ratio(2)
+        square_and_tanh(1)
+        inverse_deviation(3)
+        terms(1)
+        add_terms(0)
+        square_and_tanh(2)
+        ratio(3)
+        scale_by_unit(0, hidden01[:, 0:H])
+        terms(2)
+        add_terms(1)
+        square_and_tanh(3)
+        terms(3)
+        scale_by_unit(1, hidden01[:, H : 2 * H])
+        add_terms(2)
+        nc.scalar.activation(
+            ta_grouped[:].rearrange("p (c i j) -> p c j i", i=4, j=PACK),
+            ta_raw[:].rearrange("p j (c i) -> p c j i", i=4),
+            ACT.Copy,
+        )
+        weights["ta"] = quantise(ta_grouped[:], "ta")
+        head(hidden01[:], 0, "z01")
+        add_terms(3)
+        scale_by_unit(2, hidden2[:])
+        scale_by_unit(3, hidden3[:])
+        head(hidden2[:], 2 * P, "z2")
+        head(hidden3[:], 3 * P, "z3")

@@ -23,6 +23,8 @@ HALF_UNITS = H // 2
 HALF_TOKENS = S // 2
 BLOCKS = S // P
 LAST = BLOCKS - 1
+BANKS = {"dev": 3, "mean": 5}
+SCALAR_SHARE = 24
 
 
 def tile_picked_yadf_mean_p_kernel(tc, x_words, x_scales, w1, w2, unit, ta, offs, out):
@@ -30,7 +32,7 @@ def tile_picked_yadf_mean_p_kernel(tc, x_words, x_scales, w1, w2, unit, ta, offs
     with ExitStack() as ctx:
         keep = ctx.enter_context(tc.tile_pool(name="keep", bufs=1))
         work = ctx.enter_context(tc.tile_pool(name="work", bufs=4))
-        psum = ctx.enter_context(tc.psum_pool(name="psum", bufs=3))
+        psum = ctx.enter_context(tc.psum_pool(name="psum", bufs=1))
 
         offsets = keep.tile([P, S // 16], U16, name="offsets")
         word_window = keep.tile([P, T], I32, name="word_window", align_bytes=64)
@@ -64,10 +66,10 @@ def tile_picked_yadf_mean_p_kernel(tc, x_words, x_scales, w1, w2, unit, ta, offs
         identity = keep.tile([P, P], F32, name="identity")
         make_identity(nc, identity[:])
 
-        def cast_weights(grouped, name, c, on_scalar):
+        def cast_weights(grouped, name, c, on_scalar, first=0, last=HALF_UNITS // PACK):
             m = HALF_UNITS // PACK
-            dst = grouped[:].rearrange("p (t m j) -> p m j t", t=PACK, j=PACK)[:, c * m : (c + 1) * m]
-            src = raw[name, c][:].rearrange("p j (m t) -> p m j t", t=PACK)
+            dst = grouped[:].rearrange("p (t m j) -> p m j t", t=PACK, j=PACK)[:, c * m + first : c * m + last]
+            src = raw[name, c][:].rearrange("p j (m t) -> p m j t", t=PACK)[:, first:last]
             if on_scalar:
                 nc.scalar.activation(dst, src, ACT.Copy)
             else:
@@ -103,13 +105,14 @@ def tile_picked_yadf_mean_p_kernel(tc, x_words, x_scales, w1, w2, unit, ta, offs
         weights = {}
         grouped_dev = keep.tile([P, PACK * H], BF16, name="grouped_dev", tag="grouped", align_bytes=64)
         cast_weights(grouped_dev, "dev", 0, True)
-        cast_weights(grouped_dev, "dev", 1, False)
+        cast_weights(grouped_dev, "dev", 1, True, last=SCALAR_SHARE)
+        cast_weights(grouped_dev, "dev", 1, False, first=SCALAR_SHARE)
         weights["dev"] = quantise(grouped_dev[:], "dev")
 
         held = {}
 
         def first_layer(name, b):
-            bank = psum.tile([P, H], F32, name="bank_" + name, tag=name)
+            bank = psum.tile([P, H], F32, name="bank_" + name, tag=name, bufs=BANKS[name])
             tokens = slice((b % 2) * P, (b % 2 + 1) * P)
             if b == LAST:
                 for t in range(PACK):
@@ -132,6 +135,29 @@ def tile_picked_yadf_mean_p_kernel(tc, x_words, x_scales, w1, w2, unit, ta, offs
             first_layer("mean", b)
             nc.vector.tensor_tensor(fresh("a", b), held["mean", b], held["inv_sd", b], ALU.mult)
 
+        def deviation_copy(b):
+            nc.scalar.activation(fresh("log_var", b), held["dev", b], ACT.Copy, scale=0.8)
+
+        def exponent_on_gpsimd(b):
+            squared = keep.tile([P, P, PACK], F32, name="squared", tag="squared")
+            nc.gpsimd.tensor_tensor(squared[:], held["a", b], held["a", b], ALU.mult)
+            nc.gpsimd.tensor_tensor(fresh("arg", b), held["log_var", b], squared[:], ALU.subtract)
+
+        def tanh(b):
+            nc.scalar.activation(fresh("th", b), held["a", b], ACT.Tanh, scale=0.851)
+
+        def square(b):
+            nc.scalar.activation(fresh("a_sq", b), held["a", b], ACT.Square)
+
+        def exponent(b):
+            nc.vector.scalar_tensor_tensor(fresh("arg", b), held["a_sq", b], -1.25, held["dev", b], ALU.mult, ALU.add)
+
+        def gate(b):
+            nc.vector.scalar_tensor_tensor(fresh("gated", b), held["th", b], 1.0, held["mean", b], ALU.add, ALU.mult)
+
+        def bump(b, scale):
+            nc.scalar.activation(fresh("bump", b), held["arg", b], ACT.Exp, bias=math.log(2.0 * 0.3989), scale=scale)
+
         def square_and_tanh(b):
             nc.scalar.activation(fresh("a_sq", b), held["a", b], ACT.Square)
             nc.scalar.activation(fresh("th", b), held["a", b], ACT.Tanh, scale=0.851)
@@ -145,7 +171,7 @@ def tile_picked_yadf_mean_p_kernel(tc, x_words, x_scales, w1, w2, unit, ta, offs
             if b == LAST:
                 nc.vector.tensor_tensor(fresh("total", b), held["gated", b], held["bump", b], ALU.add)
                 return
-            turned = psum.tile([P, PACK, P], F32, name="turned", tag="turned", bufs=2)
+            turned = psum.tile([P, PACK, P], F32, name="turned", tag="mean", bufs=BANKS["mean"])
             for k, name in enumerate(("gated", "bump")):
                 columns = held[name, b].rearrange("p n t -> p (n t)")
                 for t in range(PACK):
@@ -168,7 +194,7 @@ def tile_picked_yadf_mean_p_kernel(tc, x_words, x_scales, w1, w2, unit, ta, offs
         def head(hidden, first, name):
             width = hidden.shape[1] // PACK
             quantised = quantise(hidden, name)
-            bank = psum.tile([P, width], F32, name="bank_out", tag="dev")
+            bank = psum.tile([P, width], F32, name="bank_out", tag="dev", bufs=BANKS["dev"])
             product(bank[:], weights["ta"], slice(0, N), quantised, slice(0, width))
             result = keep.tile([P, width], F32, name="result_" + name)
             nc.scalar.copy(result[:], bank[:])
@@ -178,41 +204,52 @@ def tile_picked_yadf_mean_p_kernel(tc, x_words, x_scales, w1, w2, unit, ta, offs
         hidden01 = keep.tile([P, 2 * H], BF16, name="hidden01", align_bytes=64)
         hidden2 = keep.tile([P, H], BF16, name="hidden2", align_bytes=64)
         hidden3 = keep.tile([P, H], BF16, name="hidden3", align_bytes=64)
-        ta_grouped = keep.tile([P, PACK * N], BF16, name="ta_grouped", align_bytes=64)
+        ta_grouped = keep.tile([P, PACK * N], BF16, name="ta_grouped", tag="grouped", align_bytes=64)
 
-        cast_weights(grouped_mean, "mean", 0, True)
+        cast_weights(grouped_mean, "mean", 0, False)
         cast_weights(grouped_mean, "mean", 1, False)
         weights["mean"] = quantise(grouped_mean[:], "mean")
+        nc.vector.tensor_copy(
+            ta_grouped[:].rearrange("p (c i j) -> p c j i", i=4, j=PACK),
+            ta_raw[:].rearrange("p j (c i) -> p c j i", i=4),
+        )
+        weights["ta"] = quantise(ta_grouped[:], "ta")
         inverse_deviation(0)
         inverse_deviation(1)
         inverse_deviation(2)
+        deviation_copy(0)
+        deviation_copy(2)
         ratio(0)
         ratio(1)
-        square_and_tanh(0)
-        terms(0)
         ratio(2)
-        square_and_tanh(1)
+        exponent_on_gpsimd(0)
+        exponent_on_gpsimd(2)
+        tanh(0)
+        tanh(1)
+        square(1)
         inverse_deviation(3)
-        terms(1)
-        add_terms(0)
-        square_and_tanh(2)
+        gate(0)
+        gate(1)
+        exponent(1)
         ratio(3)
-        scale_by_unit(0, hidden01[:, 0:H])
-        terms(2)
+        tanh(2)
+        gate(2)
+        bump(0, 0.5)
+        add_terms(0)
+        square(3)
+        tanh(3)
+        exponent(3)
+        gate(3)
+        bump(1, 0.4)
         add_terms(1)
-        square_and_tanh(3)
-        terms(3)
-        scale_by_unit(1, hidden01[:, H : 2 * H])
-        add_terms(2)
-        nc.scalar.activation(
-            ta_grouped[:].rearrange("p (c i j) -> p c j i", i=4, j=PACK),
-            ta_raw[:].rearrange("p j (c i) -> p c j i", i=4),
-            ACT.Copy,
-        )
-        weights["ta"] = quantise(ta_grouped[:], "ta")
-        head(hidden01[:], 0, "z01")
+        bump(3, 0.4)
+        scale_by_unit(0, hidden01[:, 0:H])
         add_terms(3)
-        scale_by_unit(2, hidden2[:])
+        bump(2, 0.5)
+        add_terms(2)
+        scale_by_unit(1, hidden01[:, H : 2 * H])
         scale_by_unit(3, hidden3[:])
-        head(hidden2[:], 2 * P, "z2")
+        head(hidden01[:], 0, "z01")
+        scale_by_unit(2, hidden2[:])
         head(hidden3[:], 3 * P, "z3")
+        head(hidden2[:], 2 * P, "z2")

@@ -35,22 +35,22 @@ def tile_picked_yadf_mean_p_kernel(tc, x_words, x_scales, w1, w2, unit, ta, offs
         psum = ctx.enter_context(tc.psum_pool(name="psum", bufs=1))
 
         offsets = keep.tile([P, S // 16], U16, name="offsets")
-        word_window = keep.tile([P, T], I32, name="word_window", align_bytes=64)
-        scale_window = keep.tile([P, T], U8, name="scale_window", align_bytes=64)
+        word_window = keep.tile([P, T], I32, name="word_window", align_bytes=256)
+        scale_window = keep.tile([P, T], U8, name="scale_window", align_bytes=256)
         nc.gpsimd.memset(scale_window[:].bitcast(I32), 0)
 
         raw = {}
 
         def load_weights(name, w):
             for c in range(2):
-                raw[name, c] = keep.tile([P, PACK, HALF_UNITS], F32, name="raw_%s%d" % (name, c))
+                raw[name, c] = keep.tile([P, PACK, HALF_UNITS], F32, name="raw_%s%d" % (name, c), align_bytes=256)
                 nc.sync.dma_start(
                     raw[name, c][:],
                     w[:, c * HALF_UNITS : (c + 1) * HALF_UNITS].rearrange("(p j) c -> p j c", j=PACK),
                 )
 
-        nc.sync.dma_start(offsets[:], offs)
         nc.sync.dma_start(word_window[:], x_words[0].rearrange("p n t -> p (n t)").bitcast(I32))
+        nc.sync.dma_start(offsets[:], offs)
         for q in range(4):
             nc.sync.dma_start(
                 scale_window[32 * q : 32 * q + 4, :].bitcast(I32),
@@ -58,7 +58,7 @@ def tile_picked_yadf_mean_p_kernel(tc, x_words, x_scales, w1, w2, unit, ta, offs
             )
         load_weights("dev", w2)
         load_weights("mean", w1)
-        ta_raw = keep.tile([P, PACK, N], F32, name="ta_raw")
+        ta_raw = keep.tile([P, PACK, N], F32, name="ta_raw", align_bytes=256)
         nc.sync.dma_start(ta_raw[:], ta.rearrange("(p j) c -> p j c", j=PACK))
         unit_raw = keep.tile([P, 1, PACK], F32, name="unit_raw")
         nc.sync.dma_start(unit_raw[:, 0, :], unit.rearrange("(p t) o -> p (t o)", t=PACK))
@@ -93,14 +93,11 @@ def tile_picked_yadf_mean_p_kernel(tc, x_words, x_scales, w1, w2, unit, ta, offs
                 stop=True,
             )
 
-        picked = []
-        for h in range(2):
-            entries = offsets[:, h * (HALF_TOKENS // 16) : (h + 1) * (HALF_TOKENS // 16)]
-            words = keep.tile([P, HALF_TOKENS], U32, name="x_codes%d" % h, align_bytes=64)
-            scales = keep.tile([P, HALF_TOKENS], U8, name="x_scales%d" % h, align_bytes=64)
-            nc.vector.tensor_copy(words[:], word_window[:].bitcast(U32).indirect(entries))
-            nc.vector.tensor_copy(scales[:], scale_window[:].indirect(entries))
-            picked.append((words, scales))
+        picked_words = keep.tile([P, S], U32, name="picked_words", align_bytes=64)
+        picked_scales = keep.tile([P, S], U8, name="picked_scales", align_bytes=64)
+        nc.vector.tensor_copy(picked_words[:], word_window[:].bitcast(U32).indirect(offsets[:]))
+        nc.vector.tensor_copy(picked_scales[:], scale_window[:].indirect(offsets[:]))
+        picked = (picked_words, picked_scales)
 
         weights = {}
         grouped_dev = keep.tile([P, PACK * H], BF16, name="grouped_dev", tag="grouped", align_bytes=64)
@@ -113,13 +110,13 @@ def tile_picked_yadf_mean_p_kernel(tc, x_words, x_scales, w1, w2, unit, ta, offs
 
         def first_layer(name, b):
             bank = psum.tile([P, H], F32, name="bank_" + name, tag=name, bufs=BANKS[name])
-            tokens = slice((b % 2) * P, (b % 2 + 1) * P)
+            tokens = slice(b * P, (b + 1) * P)
             if b == LAST:
                 for t in range(PACK):
-                    product(bank[:, t * P : (t + 1) * P], weights[name], slice(t * P, (t + 1) * P), picked[b // 2], tokens)
+                    product(bank[:, t * P : (t + 1) * P], weights[name], slice(t * P, (t + 1) * P), picked, tokens)
                 held[name, b] = bank[:].rearrange("p (t n) -> p n t", t=PACK)
             else:
-                product(bank[:], picked[b // 2], tokens, weights[name], slice(0, H))
+                product(bank[:], picked, tokens, weights[name], slice(0, H))
                 held[name, b] = bank[:].rearrange("p (n t) -> p n t", t=PACK)
 
         def fresh(name, b):
@@ -196,7 +193,7 @@ def tile_picked_yadf_mean_p_kernel(tc, x_words, x_scales, w1, w2, unit, ta, offs
             quantised = quantise(hidden, name)
             bank = psum.tile([P, width], F32, name="bank_out", tag="dev", bufs=BANKS["dev"])
             product(bank[:], weights["ta"], slice(0, N), quantised, slice(0, width))
-            result = keep.tile([P, width], F32, name="result_" + name)
+            result = keep.tile([P, width], F32, name="result_" + name, align_bytes=256)
             nc.scalar.copy(result[:], bank[:])
             nc.sync.dma_start(out[:, first : first + width], result[:])
 
@@ -206,7 +203,8 @@ def tile_picked_yadf_mean_p_kernel(tc, x_words, x_scales, w1, w2, unit, ta, offs
         hidden3 = keep.tile([P, H], BF16, name="hidden3", align_bytes=64)
         ta_grouped = keep.tile([P, PACK * N], BF16, name="ta_grouped", tag="grouped", align_bytes=64)
 
-        cast_weights(grouped_mean, "mean", 0, False)
+        cast_weights(grouped_mean, "mean", 0, True, last=SCALAR_SHARE)
+        cast_weights(grouped_mean, "mean", 0, False, first=SCALAR_SHARE)
         cast_weights(grouped_mean, "mean", 1, False)
         weights["mean"] = quantise(grouped_mean[:], "mean")
         nc.vector.tensor_copy(

import math
from contextlib import ExitStack

import concourse.mybir as mybir
from concourse.masks import make_identity

K, T, S, H, N = 512, 2048, 512, 512, 128
FLOPS = 2 * K * H * S * 2 + 2 * H * N * S

F32 = mybir.dt.float32
BF16 = mybir.dt.bfloat16
I32 = mybir.dt.int32
U32 = mybir.dt.uint32
U16 = mybir.dt.uint16
U8 = mybir.dt.uint8
FP8X4 = mybir.dt.float8_e4m3fn_x4
ACT = mybir.ActivationFunctionType
ALU = mybir.AluOpType

P = 128
PACK = 4
HALF_UNITS = H // 2
HALF_TOKENS = S // 2
BLOCKS = S // P
LAST = BLOCKS - 1
BANKS = {"dev": 3, "mean": 5}
SCALAR_SHARE = 24


def tile_picked_yadf_mean_p_kernel(tc, x_words, x_scales, w1, w2, unit, ta, offs, out):
    nc = tc.nc
    with ExitStack() as ctx:
        keep = ctx.enter_context(tc.tile_pool(name="keep", bufs=1))
        work = ctx.enter_context(tc.tile_pool(name="work", bufs=4))
        psum = ctx.enter_context(tc.psum_pool(name="psum", bufs=1))

        offsets = keep.tile([P, S // 16], U16, name="offsets")
        word_window = keep.tile([P, T], I32, name="word_window", align_bytes=256)
        scale_window = keep.tile([P, T], U8, name="scale_window", align_bytes=256)
        nc.gpsimd.memset(scale_window[:].bitcast(I32), 0)

        raw = {}

        def load_weights(name, w):
            for c in range(2):
                raw[name, c] = keep.tile([P, PACK, HALF_UNITS], F32, name="raw_%s%d" % (name, c), align_bytes=256)
                nc.sync.dma_start(
                    raw[name, c][:],
                    w[:, c * HALF_UNITS : (c + 1) * HALF_UNITS].rearrange("(p j) c -> p j c", j=PACK),
                )

        nc.sync.dma_start(word_window[:], x_words[0].rearrange("p n t -> p (n t)").bitcast(I32))
        nc.sync.dma_start(offsets[:], offs)
        for q in range(4):
            nc.sync.dma_start(
                scale_window[32 * q : 32 * q + 4, :].bitcast(I32),
                x_scales[0, 4 * q : 4 * q + 4, :].bitcast(I32),
            )
        load_weights("dev", w2)
        load_weights("mean", w1)
        ta_raw = keep.tile([P, PACK, N], F32, name="ta_raw", align_bytes=256)
        nc.sync.dma_start(ta_raw[:], ta.rearrange("(p j) c -> p j c", j=PACK))
        unit_raw = keep.tile([P, 1, PACK], F32, name="unit_raw")
        nc.sync.dma_start(unit_raw[:, 0, :], unit.rearrange("(p t) o -> p (t o)", t=PACK))

        identity = keep.tile([P, P], F32, name="identity")
        make_identity(nc, identity[:])

        def cast_weights(grouped, name, c, on_scalar, first=0, last=HALF_UNITS // PACK):
            m = HALF_UNITS // PACK
            dst = grouped[:].rearrange("p (t m j) -> p m j t", t=PACK, j=PACK)[:, c * m + first : c * m + last]
            src = raw[name, c][:].rearrange("p j (m t) -> p m j t", t=PACK)[:, first:last]
            if on_scalar:
                nc.scalar.activation(dst, src, ACT.Copy)
            else:
                nc.vector.tensor_copy(dst, src)

        def quantise(grouped, name):
            width = grouped.shape[1] // PACK
            codes = keep.tile([P, width], U32, name="codes_" + name, align_bytes=64)
            scales = keep.tile([P, width], U8, name="scales_" + name, align_bytes=64)
            nc.vector.quantize_mx(out=codes[:].bitcast(FP8X4), scales=scales[:], in_=grouped)
            return codes, scales

        def product(bank, lhs, lhs_cols, rhs, rhs_cols):
            nc.tensor.matmul_mx(
                out=bank,
                lhsT=lhs[0][:, lhs_cols].bitcast(FP8X4),
                lhsT_scale=lhs[1][:, lhs_cols],
                rhs=rhs[0][:, rhs_cols].bitcast(FP8X4),
                rhs_scale=rhs[1][:, rhs_cols],
                start=True,
                stop=True,
            )

        picked_words = keep.tile([P, S], U32, name="picked_words", align_bytes=64)
        picked_scales = keep.tile([P, S], U8, name="picked_scales", align_bytes=64)
        nc.vector.tensor_copy(picked_words[:], word_window[:].bitcast(U32).indirect(offsets[:]))
        nc.vector.tensor_copy(picked_scales[:], scale_window[:].indirect(offsets[:]))
        picked = (picked_words, picked_scales)

        weights = {}
        grouped_dev = keep.tile([P, PACK * H], BF16, name="grouped_dev", tag="grouped", align_bytes=64)
        cast_weights(grouped_dev, "dev", 0, True)
        cast_weights(grouped_dev, "dev", 1, True, last=SCALAR_SHARE)
        cast_weights(grouped_dev, "dev", 1, False, first=SCALAR_SHARE)
        weights["dev"] = quantise(grouped_dev[:], "dev")

        held = {}

        def first_layer(name, b):
            bank = psum.tile([P, H], F32, name="bank_" + name, tag=name, bufs=BANKS[name])
            tokens = slice(b * P, (b + 1) * P)
            if b == LAST:
                for t in range(PACK):
                    product(bank[:, t * P : (t + 1) * P], weights[name], slice(t * P, (t + 1) * P), picked, tokens)
                held[name, b] = bank[:].rearrange("p (t n) -> p n t", t=PACK)
            else:
                product(bank[:], picked, tokens, weights[name], slice(0, H))
                held[name, b] = bank[:].rearrange("p (n t) -> p n t", t=PACK)

        def fresh(name, b):
            tile = work.tile([P, P, PACK], F32, name=name, tag=name)
            held[name, b] = tile[:]
            return held[name, b]

        def inverse_deviation(b):
            first_layer("dev", b)
            nc.scalar.activation(fresh("inv_sd", b), held["dev", b], ACT.Exp, scale=-0.4)

        def ratio(b):
            first_layer("mean", b)
            nc.vector.tensor_tensor(fresh("a", b), held["mean", b], held["inv_sd", b], ALU.mult)

        def deviation_copy(b):
            nc.scalar.activation(fresh("log_var", b), held["dev", b], ACT.Copy, scale=0.8)

        def exponent_on_gpsimd(b):
            squared = keep.tile([P, P, PACK], F32, name="squared", tag="squared")
            nc.gpsimd.tensor_tensor(squared[:], held["a", b], held["a", b], ALU.mult)
            nc.gpsimd.tensor_tensor(fresh("arg", b), held["log_var", b], squared[:], ALU.subtract)

        def tanh(b):
            nc.scalar.activation(fresh("th", b), held["a", b], ACT.Tanh, scale=0.851)

        def square(b):
            nc.scalar.activation(fresh("a_sq", b), held["a", b], ACT.Square)

        def exponent(b):
            nc.vector.scalar_tensor_tensor(fresh("arg", b), held["a_sq", b], -1.25, held["dev", b], ALU.mult, ALU.add)

        def gate(b):
            nc.vector.scalar_tensor_tensor(fresh("gated", b), held["th", b], 1.0, held["mean", b], ALU.add, ALU.mult)

        def bump(b, scale):
            nc.scalar.activation(fresh("bump", b), held["arg", b], ACT.Exp, bias=math.log(2.0 * 0.3989), scale=scale)

        def square_and_tanh(b):
            nc.scalar.activation(fresh("a_sq", b), held["a", b], ACT.Square)
            nc.scalar.activation(fresh("th", b), held["a", b], ACT.Tanh, scale=0.851)

        def terms(b):
            nc.vector.scalar_tensor_tensor(fresh("arg", b), held["a_sq", b], -1.25, held["dev", b], ALU.mult, ALU.add)
            nc.vector.scalar_tensor_tensor(fresh("gated", b), held["th", b], 1.0, held["mean", b], ALU.add, ALU.mult)
            nc.scalar.activation(fresh("bump", b), held["arg", b], ACT.Exp, bias=math.log(2.0 * 0.3989), scale=0.4)

        def add_terms(b):
            if b == LAST:
                nc.vector.tensor_tensor(fresh("total", b), held["gated", b], held["bump", b], ALU.add)
                return
            turned = psum.tile([P, PACK, P], F32, name="turned", tag="mean", bufs=BANKS["mean"])
            for k, name in enumerate(("gated", "bump")):
                columns = held[name, b].rearrange("p n t -> p (n t)")
                for t in range(PACK):
                    nc.tensor.matmul(
                        turned[:, t, :], columns[:, t * P : (t + 1) * P], identity[:],
                        start=(k == 0 and t == 0), stop=(k == 1 and t == PACK - 1), is_transpose=True,
                    )
            held["total", b] = turned[:].rearrange("p t n -> p n t")

        def scale_by_unit(b, hidden):
            nc.vector.scalar_tensor_tensor(
                hidden.rearrange("p (n t) -> p n t", t=PACK),
                held["total", b],
                0.5,
                unit_raw[:].to_broadcast([P, P, PACK]),
                ALU.mult,
                ALU.mult,
            )

        def head(hidden, first, name):
            width = hidden.shape[1] // PACK
            quantised = quantise(hidden, name)
            bank = psum.tile([P, width], F32, name="bank_out", tag="dev", bufs=BANKS["dev"])
            product(bank[:], weights["ta"], slice(0, N), quantised, slice(0, width))
            result = keep.tile([P, width], F32, name="result_" + name, align_bytes=256)
            nc.scalar.copy(result[:], bank[:])
            nc.sync.dma_start(out[:, first : first + width], result[:])

        grouped_mean = keep.tile([P, PACK * H], BF16, name="grouped_mean", tag="grouped", align_bytes=64)
        hidden01 = keep.tile([P, 2 * H], BF16, name="hidden01", align_bytes=64)
        hidden2 = keep.tile([P, H], BF16, name="hidden2", align_bytes=64)
        hidden3 = keep.tile([P, H], BF16, name="hidden3", align_bytes=64)
        ta_grouped = keep.tile([P, PACK * N], BF16, name="ta_grouped", tag="grouped", align_bytes=64)

        cast_weights(grouped_mean, "mean", 0, True, last=SCALAR_SHARE)
        cast_weights(grouped_mean, "mean", 0, False, first=SCALAR_SHARE)
        cast_weights(grouped_mean, "mean", 1, False)
        weights["mean"] = quantise(grouped_mean[:], "mean")
        nc.vector.tensor_copy(
            ta_grouped[:].rearrange("p (c i j) -> p c j i", i=4, j=PACK),
            ta_raw[:].rearrange("p j (c i) -> p c j i", i=4),
        )
        weights["ta"] = quantise(ta_grouped[:], "ta")
        inverse_deviation(0)
        inverse_deviation(1)
        inverse_deviation(2)
        deviation_copy(0)
        deviation_copy(2)
        ratio(0)
        ratio(1)
        ratio(2)
        exponent_on_gpsimd(0)
        exponent_on_gpsimd(2)
        tanh(0)
        tanh(1)
        square(1)
        inverse_deviation(3)
        gate(0)
        gate(1)
        exponent(1)
        ratio(3)
        tanh(2)
        gate(2)
        bump(0, 0.5)
        add_terms(0)
        square(3)
        tanh(3)
        exponent(3)
        gate(3)
        bump(1, 0.4)
        add_terms(1)
        bump(3, 0.4)
        scale_by_unit(0, hidden01[:, 0:H])
        add_terms(3)
        bump(2, 0.5)
        add_terms(2)
        scale_by_unit(1, hidden01[:, H : 2 * H])
        scale_by_unit(3, hidden3[:])
        head(hidden01[:], 0, "z01")
        scale_by_unit(2, hidden2[:])
        head(hidden3[:], 3 * P, "z3")
        head(hidden2[:], 2 * P, "z2")
